import numpy as np
import ml_dtypes


def mxq(x, axis, fmt="e4m3"):
    dtype, down = {"e4m3": (ml_dtypes.float8_e4m3fn, 7), "e5m2": (ml_dtypes.float8_e5m2, 14)}[fmt]
    v = np.moveaxis(np.asarray(x, np.float32).astype(ml_dtypes.bfloat16).astype(np.float64), axis, -1)
    blocks = v.reshape(v.shape[:-1] + (-1, 32))
    amax = np.abs(blocks).max(-1, keepdims=True)
    byte = np.maximum(np.where(amax > 0, np.frexp(amax)[1] - 1 + 127, 0) - down, 1)
    scale = np.exp2(byte - 127.0)
    codes = (blocks / scale).astype(np.float32).astype(dtype).astype(np.float64)
    return np.moveaxis((codes * scale).reshape(v.shape), -1, axis)


WIDE = False


def mx_kscale(k):
    if not WIDE:
        return np.ones(k)
    levels = np.array([30, -30])
    if k % 512:
        return np.exp2(np.random.permutation(np.resize(levels, k // 32))).repeat(32)
    a = np.empty((k // 512, 16))
    for p in range(k // 512):
        a[p, :8] = np.random.permutation(np.resize(levels, 8))
        for g in range(8):
            far = levels[np.abs(levels - a[p, g]) >= 10]
            a[p, g + 8] = far[np.random.randint(len(far))]
    return np.exp2(a.ravel()).repeat(32)


def f64(x):
    return np.asarray(x).astype(np.float64)


def striped(idx):
    return np.tile(np.asarray(idx).reshape(-1, 16).T, (8, 1)).astype(np.uint16)


def unstriped(offs):
    return offs[:16].T.reshape(-1).astype(np.int64)


E2M1 = np.array([0.0, 0.5, 1.0, 1.5, 2.0, 3.0, 4.0, 6.0, -0.0, -0.5, -1.0, -1.5, -2.0, -3.0, -4.0, -6.0])


def pack_weight(w, fmt):
    k, n = w.shape
    w = f64(np.asarray(w, np.float32).astype(ml_dtypes.bfloat16)).reshape(k // 32, 32, n)
    amax = np.abs(w).max(1)
    if fmt in ("e4m3", "e5m2"):
        byte = np.frexp(amax)[1] - 1 + 127 - (7 if fmt == "e4m3" else 14)
    else:
        mant, ex = np.frexp(amax / 6.0)
        byte = np.where(mant > 0.5, ex, ex - 1) + 127
    byte = np.clip(np.where(amax > 0, byte, 1), 1, 254)
    scaled = (w * np.exp2(127.0 - byte)[:, None, :]).reshape(k, n).astype(np.float32)
    by_word = np.ascontiguousarray(scaled.reshape(k // 512, 128, 4, n).transpose(0, 1, 3, 2))
    if fmt in ("e4m3", "e5m2"):
        words = by_word.astype(ml_dtypes.float8_e4m3fn if fmt == "e4m3" else ml_dtypes.float8_e5m2).view(np.uint8)
    else:
        c = by_word.astype(ml_dtypes.float4_e2m1fn).view(np.uint8) & 0xF
        words = (c[..., 0::2] | (c[..., 1::2] << 4)).reshape(k // 512, 128, 2 * n)
    return np.ascontiguousarray(words), np.ascontiguousarray(byte.astype(np.uint8).reshape(k // 512, 16, n))


def unpack_weight(words, scales, fmt):
    g, _, n = scales.shape
    words = np.ascontiguousarray(words).reshape(g, 128, n, -1)
    if fmt in ("e4m3", "e5m2"):
        vals = words.view(ml_dtypes.float8_e4m3fn if fmt == "e4m3" else ml_dtypes.float8_e5m2).astype(np.float64)
    else:
        nib = np.empty((g, 128, n, 4), np.uint8)
        nib[..., 0::2] = words & 0xF
        nib[..., 1::2] = words >> 4
        vals = E2M1[nib]
    vals = vals * np.repeat(np.exp2(scales.astype(np.float64) - 127.0), 8, axis=1)[..., None]
    return vals.transpose(0, 1, 3, 2).reshape(g * 512, n)


K, T, J, R, O, N, E = 512, 2048, 256, 512, 128, 256, 1024


def setup_inputs():
    n = np.random.standard_normal
    idx = np.random.permutation(T)[:J]
    idx2 = np.random.permutation(T)[:J]
    idx3 = np.random.permutation(T)[:J]
    idx4 = np.random.permutation(J)[:O]
    idx5 = np.random.permutation(J)[:O]
    idx6 = np.random.permutation(E)[:O]
    fk = mx_kscale(K)
    fr = mx_kscale(R)
    xtp = pack_weight(n((K, T)) / fk[:, None], "e4m3")
    wp = pack_weight(n((K, R)) * 1 / np.sqrt(K) * fk[:, None] * fr, "e2m1")
    wbp = pack_weight(n((R, N)) * 1 / np.sqrt(R) / fr[:, None], "e5m2")
    return {
        "xt_words": xtp[0],
        "xt_scales": xtp[1],
        "w_words": wp[0],
        "w_scales": wp[1],
        "wb_words": wbp[0],
        "wb_scales": wbp[1],
        "offs": striped(idx),
        "offs2": striped(idx2),
        "offs3": striped(idx3),
        "offs4": striped(idx4),
        "offs5": striped(idx5),
        "offs6": striped(idx6),
    }


def reference(xt_words, xt_scales, w_words, w_scales, wb_words, wb_scales, offs, offs2, offs3, offs4, offs5, offs6):
    idx = unstriped(offs)
    idx2 = unstriped(offs2)
    idx3 = unstriped(offs3)
    idx4 = unstriped(offs4)
    idx5 = unstriped(offs5)
    idx6 = unstriped(offs6)
    xtu = unpack_weight(xt_words, xt_scales, "e4m3")
    wu = unpack_weight(w_words, w_scales, "e2m1")
    wbu = unpack_weight(wb_words, wb_scales, "e5m2")
    xtidxg = xtu[:, idx]
    a = wu.T @ xtidxg
    xtidx2g = xtu[:, idx2]
    b = wu.T @ xtidx2g
    xtidx3g = xtu[:, idx3]
    g0 = wu.T @ xtidx3g
    c1 = np.maximum(b, g0)
    hid = np.abs(a[:, idx4] - c1[:, idx5])
    hidq = mxq(hid, 0, "e4m3")
    p = wbu.T @ hidq
    y = np.zeros((N, E))
    y[:, idx6] = p
    return y

@@ -1,0 +1,174 @@
+from contextlib import ExitStack
+
+import concourse.mybir as mybir
+
+K, T, J, R, O, N, E = 512, 2048, 256, 512, 128, 256, 1024
+FLOPS = 3 * 2 * K * R * J + 2 * R * N * O
+
+F32 = mybir.dt.float32
+BF16 = mybir.dt.bfloat16
+I32 = mybir.dt.int32
+U32 = mybir.dt.uint32
+U16 = mybir.dt.uint16
+U8 = mybir.dt.uint8
+E4M3 = mybir.dt.float8_e4m3fn_x4
+E5M2 = mybir.dt.float8_e5m2_x4
+E2M1 = mybir.dt.float4_e2m1fn_x4
+ALU = mybir.AluOpType
+ACT = mybir.ActivationFunctionType
+
+P = 128
+PACK = 4
+SPLIT = 72
+
+
+def load_scale_rows(queues, plane, scales):
+    for q in range(4):
+        queues[q].dma_start(
+            out=plane[32 * q : 32 * q + 4, :].bitcast(I32),
+            in_=scales[0, 4 * q : 4 * q + 4, :].bitcast(I32),
+        )
+
+
+def tile_list_triple_looked_one_scattered_kernel(
+    tc, xt_words, xt_scales, w_words, w_scales, wb_words, wb_scales, offs, offs2, offs3, offs4, offs5, offs6, out
+):
+    nc = tc.nc
+    with ExitStack() as ctx:
+        keep = ctx.enter_context(tc.tile_pool(name="keep", bufs=1))
+        psum = ctx.enter_context(tc.psum_pool(name="psum", bufs=8))
+
+        list_a = keep.tile([P, J // 16], U16, name="list_a")
+        list_b = keep.tile([P, J // 16], U16, name="list_b")
+        list_g = keep.tile([P, J // 16], U16, name="list_g")
+        list_pick_a = keep.tile([P, O // 16], U16, name="list_pick_a")
+        list_pick_c = keep.tile([P, O // 16], U16, name="list_pick_c")
+        list_put = keep.tile([P, O // 16], U16, name="list_put")
+
+        x_words = keep.tile([P, T], U32, name="x_words", align_bytes=64)
+        x_plane = keep.tile([P, T], U8, name="x_plane", align_bytes=64)
+        w_raw = keep.tile([P, 2 * R], U8, name="w_raw", align_bytes=64)
+        w_plane_raw = keep.tile([P, R], U8, name="w_plane_raw", tag="raw_then_picked", align_bytes=64)
+        w_dealt = keep.tile([P, 2 * R], U8, name="w_dealt", align_bytes=64)
+        w_plane = keep.tile([P, R], U8, name="w_plane", align_bytes=64)
+        wb_codes = keep.tile([P, N], U32, name="wb_codes", align_bytes=64)
+        wb_plane = keep.tile([P, N], U8, name="wb_plane", align_bytes=64)
+        pages = [keep.tile([P, E], F32, name="page%d" % h) for h in range(2)]
+
+        nc.vector.memset(x_plane[:].bitcast(I32), 0)
+        nc.vector.memset(w_plane_raw[:].bitcast(I32), 0)
+        nc.vector.memset(wb_plane[:].bitcast(I32), 0)
+
+        nc.sync.dma_start(list_a[:], offs)
+        nc.sync.dma_start(list_b[:], offs2)
+        nc.sync.dma_start(list_g[:], offs3)
+        nc.sync.dma_start(
+            out=x_words[:].bitcast(I32), in_=xt_words[0].rearrange("p c r -> p (c r)").bitcast(I32)
+        )
+        load_scale_rows([nc.scalar] * 4, x_plane, xt_scales)
+        nc.gpsimd.dma_start(out=w_raw[:].bitcast(I32), in_=w_words[0].bitcast(I32))
+        load_scale_rows([nc.scalar] * 3 + [nc.gpsimd], w_plane_raw, w_scales)
+        nc.sync.dma_start(list_pick_a[:], offs4)
+        nc.sync.dma_start(list_pick_c[:], offs5)
+        nc.sync.dma_start(list_put[:], offs6)
+        nc.sync.dma_start(
+            out=wb_codes[:].bitcast(I32), in_=wb_words[0].rearrange("p c r -> p (c r)").bitcast(I32)
+        )
+        load_scale_rows([nc.sync] * 4, wb_plane, wb_scales)
+
+        for page in pages:
+            nc.vector.memset(page[:].bitcast(I32), 0)
+
+        lists = {"a": list_a, "b": list_b, "g": list_g}
+        picked_plane = {}
+        for name in lists:
+            picked_plane[name] = keep.tile([P, J], U8, name="plane_" + name, align_bytes=64)
+
+        for name in lists:
+            nc.vector.tensor_copy(picked_plane[name][:], x_plane[:].indirect(lists[name][:]))
+
+        nc.vector.tensor_copy(
+            out=w_dealt[:].bitcast(U16).rearrange("p (t m) -> p t m", t=PACK),
+            in_=w_raw[:].bitcast(U16).rearrange("p (m t) -> p t m", t=PACK),
+        )
+        nc.vector.tensor_copy(
+            out=w_plane[:].rearrange("p (t m) -> p t m", t=PACK),
+            in_=w_plane_raw[:].rearrange("p (m t) -> p t m", t=PACK),
+        )
+
+        picked = keep.tile([P, 3 * J], U32, name="picked", tag="raw_then_picked", align_bytes=64)
+        picked_words = {name: picked[:, J * i : J * (i + 1)] for i, name in enumerate(lists)}
+        for name in lists:
+            nc.vector.tensor_copy(picked_words[name], x_words[:].indirect(lists[name][:]))
+
+        def first_product(name, t):
+            bank = psum.tile([P, J], F32, name="bank")
+            nc.tensor.matmul_mx(
+                out=bank[:],
+                lhsT=w_dealt[:, 2 * P * t : 2 * P * (t + 1)].bitcast(E2M1),
+                lhsT_scale=w_plane[:, P * t : P * (t + 1)],
+                rhs=picked_words[name].bitcast(E4M3),
+                rhs_scale=picked_plane[name][:],
+                start=True,
+                stop=True,
+            )
+            return bank
+
+        diff = keep.tile([P, PACK, O], F32, name="diff")
+        for half in range(2):
+            slices = (2 * half, 2 * half + 1)
+            banks = {(name, t): first_product(name, t) for name in lists for t in slices}
+            whole = {}
+            for name in ("a", "b"):
+                for t in slices:
+                    whole[name, t] = keep.tile([P, J], F32, name="%s%d" % (name, t))
+                    nc.scalar.copy(out=whole[name, t][:], in_=banks[name, t][:])
+            a_picked = {t: keep.tile([P, O], F32, name="a_picked%d" % t) for t in slices}
+            for t in slices:
+                window = whole["a", t][:].indirect(list_pick_a[:])
+                if half == 0:
+                    nc.vector.tensor_copy(a_picked[t][:], window)
+                else:
+                    nc.scalar.activation(a_picked[t][:], window, ACT.Copy)
+            c1 = {t: keep.tile([P, J], F32, name="c1_%d" % t) for t in slices}
+            for t in slices:
+                nc.vector.tensor_tensor(c1[t][:], banks["g", t][:], whole["b", t][:], ALU.max)
+            for t in slices:
+                nc.vector.tensor_tensor(
+                    diff[:, t, :], c1[t][:].indirect(list_pick_c[:]), a_picked[t][:], ALU.subtract
+                )
+
+        hid = keep.tile([P, O, PACK], BF16, name="hid", align_bytes=64)
+        nc.scalar.activation(
+            hid[:, 0:SPLIT, :].rearrange("p (c i) t -> p c t i", i=4),
+            diff[:, :, 0:SPLIT].rearrange("p t (c i) -> p c t i", i=4),
+            ACT.Abs,
+        )
+        rest = diff[:, :, SPLIT:O].rearrange("p t o -> p o t")
+        nc.vector.scalar_tensor_tensor(hid[:, SPLIT:O, :], rest, -1.0, rest, ALU.mult, ALU.max)
+        hid_codes = keep.tile([P, O], U32, name="hid_codes", align_bytes=64)
+        hid_plane = keep.tile([P, O], U8, name="hid_plane", align_bytes=64)
+        nc.vector.quantize_mx(
+            out=hid_codes[:].bitcast(E4M3), scales=hid_plane[:], in_=hid[:].rearrange("p o t -> p (o t)")
+        )
+
+        for h in range(2):
+            bank_p = psum.tile([P, O], F32, name="bank")
+            nc.tensor.matmul_mx(
+                out=bank_p[:],
+                lhsT=wb_codes[:, P * h : P * (h + 1)].bitcast(E5M2),
+                lhsT_scale=wb_plane[:, P * h : P * (h + 1)],
+                rhs=hid_codes[:].bitcast(E4M3),
+                rhs_scale=hid_plane[:],
+                start=True,
+                stop=True,
+            )
+            p_sb = keep.tile([P, O], F32, name="p_sb%d" % h)
+            if h == 0:
+                nc.vector.tensor_copy(p_sb[:], bank_p[:])
+                nc.vector.tensor_copy(pages[h][:].indirect(list_put[:]), p_sb[:])
+                nc.sync.dma_start(out=out[P * h : P * (h + 1), :], in_=pages[h][:])
+            else:
+                nc.scalar.copy(p_sb[:], bank_p[:])
+                nc.scalar.activation(pages[h][:].indirect(list_put[:]), p_sb[:], ACT.Copy)
+                nc.scalar.dma_start(out=out[P * h : P * (h + 1), :], in_=pages[h][:])

@@ -19,12 +19,11 @@ ACT = mybir.ActivationFunctionType
 
 P = 128
 PACK = 4
-SPLIT = 72
 
 
-def load_scale_rows(queues, plane, scales):
-    for q in range(4):
-        queues[q].dma_start(
+def load_scale_rows(queue, plane, scales, quadrants):
+    for q in quadrants:
+        queue.dma_start(
             out=plane[32 * q : 32 * q + 4, :].bitcast(I32),
             in_=scales[0, 4 * q : 4 * q + 4, :].bitcast(I32),
         )
@@ -56,28 +55,28 @@ def tile_list_triple_looked_one_scattered_kernel(
         pages = [keep.tile([P, E], F32, name="page%d" % h) for h in range(2)]
 
         nc.vector.memset(x_plane[:].bitcast(I32), 0)
+        for page in pages:
+            nc.vector.memset(page[:].bitcast(I32), 0)
         nc.vector.memset(w_plane_raw[:].bitcast(I32), 0)
         nc.vector.memset(wb_plane[:].bitcast(I32), 0)
 
         nc.sync.dma_start(list_a[:], offs)
         nc.sync.dma_start(list_b[:], offs2)
+        load_scale_rows(nc.scalar, x_plane, xt_scales, (0, 1))
+        load_scale_rows(nc.sync, x_plane, xt_scales, (2, 3))
         nc.sync.dma_start(list_g[:], offs3)
         nc.sync.dma_start(
             out=x_words[:].bitcast(I32), in_=xt_words[0].rearrange("p c r -> p (c r)").bitcast(I32)
         )
-        load_scale_rows([nc.scalar] * 4, x_plane, xt_scales)
         nc.gpsimd.dma_start(out=w_raw[:].bitcast(I32), in_=w_words[0].bitcast(I32))
-        load_scale_rows([nc.scalar] * 3 + [nc.gpsimd], w_plane_raw, w_scales)
+        load_scale_rows(nc.scalar, w_plane_raw, w_scales, range(4))
         nc.sync.dma_start(list_pick_a[:], offs4)
         nc.sync.dma_start(list_pick_c[:], offs5)
         nc.sync.dma_start(list_put[:], offs6)
         nc.sync.dma_start(
             out=wb_codes[:].bitcast(I32), in_=wb_words[0].rearrange("p c r -> p (c r)").bitcast(I32)
         )
-        load_scale_rows([nc.sync] * 4, wb_plane, wb_scales)
-
-        for page in pages:
-            nc.vector.memset(page[:].bitcast(I32), 0)
+        load_scale_rows(nc.sync, wb_plane, wb_scales, range(4))
 
         lists = {"a": list_a, "b": list_b, "g": list_g}
         picked_plane = {}
@@ -115,6 +114,17 @@ def tile_list_triple_looked_one_scattered_kernel(
             return bank
 
         diff = keep.tile([P, PACK, O], F32, name="diff")
+        a_picked = {t: keep.tile([P, O], F32, name="a_picked%d" % t) for t in range(PACK)}
+        c1 = {t: keep.tile([P, J], F32, name="c1_%d" % t) for t in range(PACK)}
+
+        def subtract_picked(t, lo, hi):
+            nc.vector.tensor_tensor(
+                diff[:, t, lo:hi],
+                c1[t][:].indirect(list_pick_c[:, lo // 16 : hi // 16]),
+                a_picked[t][:, lo:hi],
+                ALU.subtract,
+            )
+
         for half in range(2):
             slices = (2 * half, 2 * half + 1)
             banks = {(name, t): first_product(name, t) for name in lists for t in slices}
@@ -123,39 +133,42 @@ def tile_list_triple_looked_one_scattered_kernel(
                 for t in slices:
                     whole[name, t] = keep.tile([P, J], F32, name="%s%d" % (name, t))
                     nc.scalar.copy(out=whole[name, t][:], in_=banks[name, t][:])
-            a_picked = {t: keep.tile([P, O], F32, name="a_picked%d" % t) for t in slices}
             for t in slices:
                 window = whole["a", t][:].indirect(list_pick_a[:])
                 if half == 0:
                     nc.vector.tensor_copy(a_picked[t][:], window)
                 else:
                     nc.scalar.activation(a_picked[t][:], window, ACT.Copy)
-            c1 = {t: keep.tile([P, J], F32, name="c1_%d" % t) for t in slices}
             for t in slices:
                 nc.vector.tensor_tensor(c1[t][:], banks["g", t][:], whole["b", t][:], ALU.max)
-            for t in slices:
-                nc.vector.tensor_tensor(
-                    diff[:, t, :], c1[t][:].indirect(list_pick_c[:]), a_picked[t][:], ALU.subtract
-                )
+            if half == 0:
+                for t in slices:
+                    subtract_picked(t, 0, O)
 
         hid = keep.tile([P, O, PACK], BF16, name="hid", align_bytes=64)
-        nc.scalar.activation(
-            hid[:, 0:SPLIT, :].rearrange("p (c i) t -> p c t i", i=4),
-            diff[:, :, 0:SPLIT].rearrange("p t (c i) -> p c t i", i=4),
-            ACT.Abs,
-        )
-        rest = diff[:, :, SPLIT:O].rearrange("p t o -> p o t")
-        nc.vector.scalar_tensor_tensor(hid[:, SPLIT:O, :], rest, -1.0, rest, ALU.mult, ALU.max)
         hid_codes = keep.tile([P, O], U32, name="hid_codes", align_bytes=64)
         hid_plane = keep.tile([P, O], U8, name="hid_plane", align_bytes=64)
-        nc.vector.quantize_mx(
-            out=hid_codes[:].bitcast(E4M3), scales=hid_plane[:], in_=hid[:].rearrange("p o t -> p (o t)")
-        )
+        parts = ((0, O // 2), (O // 2, O))
+        for lo, hi in parts:
+            for t in (2, 3):
+                subtract_picked(t, lo, hi)
+            nc.scalar.activation(
+                hid[:, lo:hi, :].rearrange("p (c i) t -> p c t i", i=4),
+                diff[:, :, lo:hi].rearrange("p t (c i) -> p c t i", i=4),
+                ACT.Abs,
+            )
+        for lo, hi in parts:
+            nc.vector.quantize_mx(
+                out=hid_codes[:, lo:hi].bitcast(E4M3),
+                scales=hid_plane[:, lo:hi],
+                in_=hid[:, lo:hi, :].rearrange("p o t -> p (o t)"),
+            )
 
-        for h in range(2):
-            bank_p = psum.tile([P, O], F32, name="bank")
+        placed = []
+        for h, empty_bank in enumerate((nc.scalar.copy, nc.vector.tensor_copy)):
+            bank = psum.tile([P, O], F32, name="bank")
             nc.tensor.matmul_mx(
-                out=bank_p[:],
+                out=bank[:],
                 lhsT=wb_codes[:, P * h : P * (h + 1)].bitcast(E5M2),
                 lhsT_scale=wb_plane[:, P * h : P * (h + 1)],
                 rhs=hid_codes[:].bitcast(E4M3),
@@ -163,12 +176,9 @@ def tile_list_triple_looked_one_scattered_kernel(
                 start=True,
                 stop=True,
             )
-            p_sb = keep.tile([P, O], F32, name="p_sb%d" % h)
-            if h == 0:
-                nc.vector.tensor_copy(p_sb[:], bank_p[:])
-                nc.vector.tensor_copy(pages[h][:].indirect(list_put[:]), p_sb[:])
-                nc.sync.dma_start(out=out[P * h : P * (h + 1), :], in_=pages[h][:])
-            else:
-                nc.scalar.copy(p_sb[:], bank_p[:])
-                nc.scalar.activation(pages[h][:].indirect(list_put[:]), p_sb[:], ACT.Copy)
-                nc.scalar.dma_start(out=out[P * h : P * (h + 1), :], in_=pages[h][:])
+            placed.append(keep.tile([P, O], F32, name="placed%d" % h))
+            empty_bank(placed[h][:], bank[:])
+        nc.vector.tensor_copy(pages[0][:].indirect(list_put[:]), placed[0][:])
+        nc.scalar.activation(pages[1][:].indirect(list_put[:]), placed[1][:], ACT.Copy)
+        nc.sync.dma_start(out=out[0:P, :], in_=pages[0][:])
+        nc.scalar.dma_start(out=out[P : 2 * P, :], in_=pages[1][:])

@@ -44,7 +44,7 @@ def tile_list_triple_looked_one_scattered_kernel(
         list_pick_c = keep.tile([P, O // 16], U16, name="list_pick_c")
         list_put = keep.tile([P, O // 16], U16, name="list_put")
 
-        x_words = keep.tile([P, T], U32, name="x_words", align_bytes=64)
+        x_words = keep.tile([P, T], U32, name="x_words", tag="table_then_page", align_bytes=64)
         x_plane = keep.tile([P, T], U8, name="x_plane", align_bytes=64)
         w_raw = keep.tile([P, 2 * R], U8, name="w_raw", align_bytes=64)
         w_plane_raw = keep.tile([P, R], U8, name="w_plane_raw", tag="raw_then_picked", align_bytes=64)
@@ -52,24 +52,23 @@ def tile_list_triple_looked_one_scattered_kernel(
         w_plane = keep.tile([P, R], U8, name="w_plane", align_bytes=64)
         wb_codes = keep.tile([P, N], U32, name="wb_codes", align_bytes=64)
         wb_plane = keep.tile([P, N], U8, name="wb_plane", align_bytes=64)
-        pages = [keep.tile([P, E], F32, name="page%d" % h) for h in range(2)]
+        page_low = keep.tile([P, E], F32, name="page_low")
 
         nc.vector.memset(x_plane[:].bitcast(I32), 0)
-        for page in pages:
-            nc.vector.memset(page[:].bitcast(I32), 0)
+        nc.vector.memset(page_low[:].bitcast(I32), 0)
         nc.vector.memset(w_plane_raw[:].bitcast(I32), 0)
         nc.vector.memset(wb_plane[:].bitcast(I32), 0)
 
         nc.sync.dma_start(list_a[:], offs)
+        nc.scalar.dma_start(out=w_raw[:].bitcast(I32), in_=w_words[0].bitcast(I32))
         nc.sync.dma_start(list_b[:], offs2)
         load_scale_rows(nc.scalar, x_plane, xt_scales, (0, 1))
         load_scale_rows(nc.sync, x_plane, xt_scales, (2, 3))
-        nc.sync.dma_start(list_g[:], offs3)
         nc.sync.dma_start(
             out=x_words[:].bitcast(I32), in_=xt_words[0].rearrange("p c r -> p (c r)").bitcast(I32)
         )
-        nc.gpsimd.dma_start(out=w_raw[:].bitcast(I32), in_=w_words[0].bitcast(I32))
         load_scale_rows(nc.scalar, w_plane_raw, w_scales, range(4))
+        nc.sync.dma_start(list_g[:], offs3)
         nc.sync.dma_start(list_pick_a[:], offs4)
         nc.sync.dma_start(list_pick_c[:], offs5)
         nc.sync.dma_start(list_put[:], offs6)
@@ -79,17 +78,17 @@ def tile_list_triple_looked_one_scattered_kernel(
         load_scale_rows(nc.sync, wb_plane, wb_scales, range(4))
 
         lists = {"a": list_a, "b": list_b, "g": list_g}
-        picked_plane = {}
-        for name in lists:
-            picked_plane[name] = keep.tile([P, J], U8, name="plane_" + name, align_bytes=64)
+        picked_plane = {name: keep.tile([P, J], U8, name="plane_" + name, align_bytes=64) for name in lists}
 
-        for name in lists:
+        def pick_scales(name):
             nc.vector.tensor_copy(picked_plane[name][:], x_plane[:].indirect(lists[name][:]))
 
         nc.vector.tensor_copy(
             out=w_dealt[:].bitcast(U16).rearrange("p (t m) -> p t m", t=PACK),
             in_=w_raw[:].bitcast(U16).rearrange("p (m t) -> p t m", t=PACK),
         )
+        pick_scales("a")
+        pick_scales("b")
         nc.vector.tensor_copy(
             out=w_plane[:].rearrange("p (t m) -> p t m", t=PACK),
             in_=w_plane_raw[:].rearrange("p (m t) -> p t m", t=PACK),
@@ -97,8 +96,14 @@ def tile_list_triple_looked_one_scattered_kernel(
 
         picked = keep.tile([P, 3 * J], U32, name="picked", tag="raw_then_picked", align_bytes=64)
         picked_words = {name: picked[:, J * i : J * (i + 1)] for i, name in enumerate(lists)}
-        for name in lists:
+
+        def pick_words(name):
             nc.vector.tensor_copy(picked_words[name], x_words[:].indirect(lists[name][:]))
+
+        pick_words("a")
+        pick_words("b")
+        pick_scales("g")
+        pick_words("g")
 
         def first_product(name, t):
             bank = psum.tile([P, J], F32, name="bank")
@@ -125,32 +130,45 @@ def tile_list_triple_looked_one_scattered_kernel(
                 ALU.subtract,
             )
 
-        for half in range(2):
-            slices = (2 * half, 2 * half + 1)
-            banks = {(name, t): first_product(name, t) for name in lists for t in slices}
-            whole = {}
-            for name in ("a", "b"):
-                for t in slices:
-                    whole[name, t] = keep.tile([P, J], F32, name="%s%d" % (name, t))
-                    nc.scalar.copy(out=whole[name, t][:], in_=banks[name, t][:])
+        early, late = (0, 1), (2, 3)
+        whole = {}
+
+        def product_in_sbuf(name, slices):
+            banks = {t: first_product(name, t) for t in slices}
             for t in slices:
-                window = whole["a", t][:].indirect(list_pick_a[:])
-                if half == 0:
-                    nc.vector.tensor_copy(a_picked[t][:], window)
-                else:
-                    nc.scalar.activation(a_picked[t][:], window, ACT.Copy)
+                whole[name, t] = keep.tile([P, J], F32, name="%s%d" % (name, t))
+                nc.scalar.copy(out=whole[name, t][:], in_=banks[t][:])
+
+        def pick_a(slices):
             for t in slices:
-                nc.vector.tensor_tensor(c1[t][:], banks["g", t][:], whole["b", t][:], ALU.max)
-            if half == 0:
-                for t in slices:
-                    subtract_picked(t, 0, O)
+                nc.scalar.activation(a_picked[t][:], whole["a", t][:].indirect(list_pick_a[:]), ACT.Copy)
+
+        def larger_of_b_and_g(slices):
+            banks = {t: first_product("g", t) for t in slices}
+            for t in slices:
+                nc.vector.tensor_tensor(c1[t][:], banks[t][:], whole["b", t][:], ALU.max)
+
+        product_in_sbuf("a", early)
+        product_in_sbuf("b", early)
+        pick_a(early)
+        product_in_sbuf("a", late)
+        larger_of_b_and_g(early)
+        for t in early:
+            subtract_picked(t, 0, O)
+        product_in_sbuf("b", late)
+        pick_a(late)
+        larger_of_b_and_g(late)
+
+        page_high = keep.tile([P, E], F32, name="page_high", tag="table_then_page", align_bytes=64)
+        nc.gpsimd.memset(page_high[:], 0.0)
+        pages = (page_low, page_high)
 
         hid = keep.tile([P, O, PACK], BF16, name="hid", align_bytes=64)
         hid_codes = keep.tile([P, O], U32, name="hid_codes", align_bytes=64)
         hid_plane = keep.tile([P, O], U8, name="hid_plane", align_bytes=64)
         parts = ((0, O // 2), (O // 2, O))
         for lo, hi in parts:
-            for t in (2, 3):
+            for t in late:
                 subtract_picked(t, lo, hi)
             nc.scalar.activation(
                 hid[:, lo:hi, :].rearrange("p (c i) t -> p c t i", i=4),

@@ -44,7 +44,7 @@ def tile_list_triple_looked_one_scattered_kernel(
         list_pick_c = keep.tile([P, O // 16], U16, name="list_pick_c")
         list_put = keep.tile([P, O // 16], U16, name="list_put")
 
-        x_words = keep.tile([P, T], U32, name="x_words", tag="table_then_page", align_bytes=64)
+        x_words = keep.tile([P, T], U32, name="x_words", align_bytes=64)
         x_plane = keep.tile([P, T], U8, name="x_plane", align_bytes=64)
         w_raw = keep.tile([P, 2 * R], U8, name="w_raw", align_bytes=64)
         w_plane_raw = keep.tile([P, R], U8, name="w_plane_raw", tag="raw_then_picked", align_bytes=64)
@@ -52,12 +52,13 @@ def tile_list_triple_looked_one_scattered_kernel(
         w_plane = keep.tile([P, R], U8, name="w_plane", align_bytes=64)
         wb_codes = keep.tile([P, N], U32, name="wb_codes", align_bytes=64)
         wb_plane = keep.tile([P, N], U8, name="wb_plane", align_bytes=64)
-        page_low = keep.tile([P, E], F32, name="page_low")
+        pages = [keep.tile([P, E], F32, name="page%d" % h) for h in range(2)]
 
         nc.vector.memset(x_plane[:].bitcast(I32), 0)
-        nc.vector.memset(page_low[:].bitcast(I32), 0)
+        nc.vector.memset(pages[0][:].bitcast(I32), 0)
         nc.vector.memset(w_plane_raw[:].bitcast(I32), 0)
         nc.vector.memset(wb_plane[:].bitcast(I32), 0)
+        nc.vector.memset(pages[1][:].bitcast(I32), 0)
 
         nc.sync.dma_start(list_a[:], offs)
         nc.scalar.dma_start(out=w_raw[:].bitcast(I32), in_=w_words[0].bitcast(I32))
@@ -89,21 +90,17 @@ def tile_list_triple_looked_one_scattered_kernel(
         )
         pick_scales("a")
         pick_scales("b")
+        words_a = keep.tile([P, J], U32, name="words_a", align_bytes=64)
+        nc.vector.tensor_copy(words_a[:], x_words[:].indirect(list_a[:]))
         nc.vector.tensor_copy(
             out=w_plane[:].rearrange("p (t m) -> p t m", t=PACK),
             in_=w_plane_raw[:].rearrange("p (m t) -> p t m", t=PACK),
         )
-
-        picked = keep.tile([P, 3 * J], U32, name="picked", tag="raw_then_picked", align_bytes=64)
-        picked_words = {name: picked[:, J * i : J * (i + 1)] for i, name in enumerate(lists)}
-
-        def pick_words(name):
-            nc.vector.tensor_copy(picked_words[name], x_words[:].indirect(lists[name][:]))
-
-        pick_words("a")
-        pick_words("b")
+        words_bg = keep.tile([P, 2 * J], U32, name="words_bg", tag="raw_then_picked", align_bytes=64)
+        picked_words = {"a": words_a[:], "b": words_bg[:, 0:J], "g": words_bg[:, J : 2 * J]}
+        nc.vector.tensor_copy(picked_words["b"], x_words[:].indirect(list_b[:]))
         pick_scales("g")
-        pick_words("g")
+        nc.vector.tensor_copy(picked_words["g"], x_words[:].indirect(list_g[:]))
 
         def first_product(name, t):
             bank = psum.tile([P, J], F32, name="bank")
@@ -158,10 +155,6 @@ def tile_list_triple_looked_one_scattered_kernel(
         product_in_sbuf("b", late)
         pick_a(late)
         larger_of_b_and_g(late)
-
-        page_high = keep.tile([P, E], F32, name="page_high", tag="table_then_page", align_bytes=64)
-        nc.gpsimd.memset(page_high[:], 0.0)
-        pages = (page_low, page_high)
 
         hid = keep.tile([P, O, PACK], BF16, name="hid", align_bytes=64)
         hid_codes = keep.tile([P, O], U32, name="hid_codes", align_bytes=64)

from contextlib import ExitStack

import concourse.mybir as mybir

K, T, J, R, O, N, E = 512, 2048, 256, 512, 128, 256, 1024
FLOPS = 3 * 2 * K * R * J + 2 * R * N * O

F32 = mybir.dt.float32
BF16 = mybir.dt.bfloat16
I32 = mybir.dt.int32
U32 = mybir.dt.uint32
U16 = mybir.dt.uint16
U8 = mybir.dt.uint8
E4M3 = mybir.dt.float8_e4m3fn_x4
E5M2 = mybir.dt.float8_e5m2_x4
E2M1 = mybir.dt.float4_e2m1fn_x4
ALU = mybir.AluOpType
ACT = mybir.ActivationFunctionType

P = 128
PACK = 4


def load_scale_rows(queue, plane, scales, quadrants):
    for q in quadrants:
        queue.dma_start(
            out=plane[32 * q : 32 * q + 4, :].bitcast(I32),
            in_=scales[0, 4 * q : 4 * q + 4, :].bitcast(I32),
        )


def tile_list_triple_looked_one_scattered_kernel(
    tc, xt_words, xt_scales, w_words, w_scales, wb_words, wb_scales, offs, offs2, offs3, offs4, offs5, offs6, out
):
    nc = tc.nc
    with ExitStack() as ctx:
        keep = ctx.enter_context(tc.tile_pool(name="keep", bufs=1))
        psum = ctx.enter_context(tc.psum_pool(name="psum", bufs=8))

        list_a = keep.tile([P, J // 16], U16, name="list_a")
        list_b = keep.tile([P, J // 16], U16, name="list_b")
        list_g = keep.tile([P, J // 16], U16, name="list_g")
        list_pick_a = keep.tile([P, O // 16], U16, name="list_pick_a")
        list_pick_c = keep.tile([P, O // 16], U16, name="list_pick_c")
        list_put = keep.tile([P, O // 16], U16, name="list_put")

        x_words = keep.tile([P, T], U32, name="x_words", align_bytes=64)
        x_plane = keep.tile([P, T], U8, name="x_plane", align_bytes=64)
        w_raw = keep.tile([P, 2 * R], U8, name="w_raw", align_bytes=64)
        w_plane_raw = keep.tile([P, R], U8, name="w_plane_raw", tag="raw_then_picked", align_bytes=64)
        w_dealt = keep.tile([P, 2 * R], U8, name="w_dealt", align_bytes=64)
        w_plane = keep.tile([P, R], U8, name="w_plane", align_bytes=64)
        wb_codes = keep.tile([P, N], U32, name="wb_codes", align_bytes=64)
        wb_plane = keep.tile([P, N], U8, name="wb_plane", align_bytes=64)
        pages = [keep.tile([P, E], F32, name="page%d" % h) for h in range(2)]

        nc.vector.memset(x_plane[:].bitcast(I32), 0)
        nc.vector.memset(pages[0][:].bitcast(I32), 0)
        nc.vector.memset(w_plane_raw[:].bitcast(I32), 0)
        nc.vector.memset(wb_plane[:].bitcast(I32), 0)
        nc.vector.memset(pages[1][:].bitcast(I32), 0)

        nc.sync.dma_start(list_a[:], offs)
        nc.scalar.dma_start(out=w_raw[:].bitcast(I32), in_=w_words[0].bitcast(I32))
        nc.sync.dma_start(list_b[:], offs2)
        load_scale_rows(nc.scalar, x_plane, xt_scales, (0, 1))
        load_scale_rows(nc.sync, x_plane, xt_scales, (2, 3))
        nc.sync.dma_start(
            out=x_words[:].bitcast(I32), in_=xt_words[0].rearrange("p c r -> p (c r)").bitcast(I32)
        )
        load_scale_rows(nc.scalar, w_plane_raw, w_scales, range(4))
        nc.sync.dma_start(list_g[:], offs3)
        nc.sync.dma_start(list_pick_a[:], offs4)
        nc.sync.dma_start(list_pick_c[:], offs5)
        nc.sync.dma_start(list_put[:], offs6)
        nc.sync.dma_start(
            out=wb_codes[:].bitcast(I32), in_=wb_words[0].rearrange("p c r -> p (c r)").bitcast(I32)
        )
        load_scale_rows(nc.sync, wb_plane, wb_scales, range(4))

        lists = {"a": list_a, "b": list_b, "g": list_g}
        picked_plane = {name: keep.tile([P, J], U8, name="plane_" + name, align_bytes=64) for name in lists}

        def pick_scales(name):
            nc.vector.tensor_copy(picked_plane[name][:], x_plane[:].indirect(lists[name][:]))

        nc.vector.tensor_copy(
            out=w_dealt[:].bitcast(U16).rearrange("p (t m) -> p t m", t=PACK),
            in_=w_raw[:].bitcast(U16).rearrange("p (m t) -> p t m", t=PACK),
        )
        pick_scales("a")
        pick_scales("b")
        words_a = keep.tile([P, J], U32, name="words_a", align_bytes=64)
        nc.vector.tensor_copy(words_a[:], x_words[:].indirect(list_a[:]))
        nc.vector.tensor_copy(
            out=w_plane[:].rearrange("p (t m) -> p t m", t=PACK),
            in_=w_plane_raw[:].rearrange("p (m t) -> p t m", t=PACK),
        )
        words_bg = keep.tile([P, 2 * J], U32, name="words_bg", tag="raw_then_picked", align_bytes=64)
        picked_words = {"a": words_a[:], "b": words_bg[:, 0:J], "g": words_bg[:, J : 2 * J]}
        nc.vector.tensor_copy(picked_words["b"], x_words[:].indirect(list_b[:]))
        pick_scales("g")
        nc.vector.tensor_copy(picked_words["g"], x_words[:].indirect(list_g[:]))

        def first_product(name, t):
            bank = psum.tile([P, J], F32, name="bank")
            nc.tensor.matmul_mx(
                out=bank[:],
                lhsT=w_dealt[:, 2 * P * t : 2 * P * (t + 1)].bitcast(E2M1),
                lhsT_scale=w_plane[:, P * t : P * (t + 1)],
                rhs=picked_words[name].bitcast(E4M3),
                rhs_scale=picked_plane[name][:],
                start=True,
                stop=True,
            )
            return bank

        diff = keep.tile([P, PACK, O], F32, name="diff")
        a_picked = {t: keep.tile([P, O], F32, name="a_picked%d" % t) for t in range(PACK)}
        c1 = {t: keep.tile([P, J], F32, name="c1_%d" % t) for t in range(PACK)}

        def subtract_picked(t, lo, hi):
            nc.vector.tensor_tensor(
                diff[:, t, lo:hi],
                c1[t][:].indirect(list_pick_c[:, lo // 16 : hi // 16]),
                a_picked[t][:, lo:hi],
                ALU.subtract,
            )

        early, late = (0, 1), (2, 3)
        whole = {}

        def product_in_sbuf(name, slices):
            banks = {t: first_product(name, t) for t in slices}
            for t in slices:
                whole[name, t] = keep.tile([P, J], F32, name="%s%d" % (name, t))
                nc.scalar.copy(out=whole[name, t][:], in_=banks[t][:])

        def pick_a(slices):
            for t in slices:
                nc.scalar.activation(a_picked[t][:], whole["a", t][:].indirect(list_pick_a[:]), ACT.Copy)

        def larger_of_b_and_g(slices):
            banks = {t: first_product("g", t) for t in slices}
            for t in slices:
                nc.vector.tensor_tensor(c1[t][:], banks[t][:], whole["b", t][:], ALU.max)

        product_in_sbuf("a", early)
        product_in_sbuf("b", early)
        pick_a(early)
        product_in_sbuf("a", late)
        larger_of_b_and_g(early)
        for t in early:
            subtract_picked(t, 0, O)
        product_in_sbuf("b", late)
        pick_a(late)
        larger_of_b_and_g(late)

        hid = keep.tile([P, O, PACK], BF16, name="hid", align_bytes=64)
        hid_codes = keep.tile([P, O], U32, name="hid_codes", align_bytes=64)
        hid_plane = keep.tile([P, O], U8, name="hid_plane", align_bytes=64)
        parts = ((0, O // 2), (O // 2, O))
        for lo, hi in parts:
            for t in late:
                subtract_picked(t, lo, hi)
            nc.scalar.activation(
                hid[:, lo:hi, :].rearrange("p (c i) t -> p c t i", i=4),
                diff[:, :, lo:hi].rearrange("p t (c i) -> p c t i", i=4),
                ACT.Abs,
            )
        for lo, hi in parts:
            nc.vector.quantize_mx(
                out=hid_codes[:, lo:hi].bitcast(E4M3),
                scales=hid_plane[:, lo:hi],
                in_=hid[:, lo:hi, :].rearrange("p o t -> p (o t)"),
            )

        placed = []
        for h, empty_bank in enumerate((nc.scalar.copy, nc.vector.tensor_copy)):
            bank = psum.tile([P, O], F32, name="bank")
            nc.tensor.matmul_mx(
                out=bank[:],
                lhsT=wb_codes[:, P * h : P * (h + 1)].bitcast(E5M2),
                lhsT_scale=wb_plane[:, P * h : P * (h + 1)],
                rhs=hid_codes[:].bitcast(E4M3),
                rhs_scale=hid_plane[:],
                start=True,
                stop=True,
            )
            placed.append(keep.tile([P, O], F32, name="placed%d" % h))
            empty_bank(placed[h][:], bank[:])
        nc.vector.tensor_copy(pages[0][:].indirect(list_put[:]), placed[0][:])
        nc.scalar.activation(pages[1][:].indirect(list_put[:]), placed[1][:], ACT.Copy)
        nc.sync.dma_start(out=out[0:P, :], in_=pages[0][:])
        nc.scalar.dma_start(out=out[P : 2 * P, :], in_=pages[1][:])
